import numpy as np
import ml_dtypes


def mxq(x, axis, fmt="e4m3"):
    dtype, down = {"e4m3": (ml_dtypes.float8_e4m3fn, 7), "e5m2": (ml_dtypes.float8_e5m2, 14)}[fmt]
    v = np.moveaxis(np.asarray(x, np.float32).astype(ml_dtypes.bfloat16).astype(np.float64), axis, -1)
    blocks = v.reshape(v.shape[:-1] + (-1, 32))
    amax = np.abs(blocks).max(-1, keepdims=True)
    byte = np.maximum(np.where(amax > 0, np.frexp(amax)[1] - 1 + 127, 0) - down, 1)
    scale = np.exp2(byte - 127.0)
    codes = (blocks / scale).astype(np.float32).astype(dtype).astype(np.float64)
    return np.moveaxis((codes * scale).reshape(v.shape), -1, axis)


WIDE = False


def mx_kscale(k):
    if not WIDE:
        return np.ones(k)
    levels = np.array([10, -10, 5, -5, 0])
    if k % 512:
        return np.exp2(np.random.permutation(np.resize(levels, k // 32))).repeat(32)
    a = np.empty((k // 512, 16))
    for p in range(k // 512):
        a[p, :8] = np.random.permutation(np.resize(levels, 8))
        for g in range(8):
            far = levels[np.abs(levels - a[p, g]) >= 10]
            a[p, g + 8] = far[np.random.randint(len(far))]
    return np.exp2(a.ravel()).repeat(32)


def f64(x):
    return np.asarray(x).astype(np.float64)


def striped(idx):
    return np.tile(idx.reshape(-1, 16).T, (8, 1)).astype(np.uint16)


def unstriped(offs):
    return offs[:16].T.reshape(-1).astype(np.int64)


def pack_weight(w):
    k, n = w.shape
    w = f64(np.asarray(w, np.float32).astype(ml_dtypes.bfloat16)).reshape(k // 32, 32, n)
    amax = np.abs(w).max(1)
    byte = np.clip(np.where(amax > 0, np.frexp(amax)[1] - 1 + 127 - 7, 1), 1, 254)
    scaled = (w * np.exp2(127.0 - byte)[:, None, :]).reshape(k, n).astype(np.float32)
    words = np.ascontiguousarray(scaled.reshape(k // 512, 128, 4, n).transpose(0, 1, 3, 2)).astype(ml_dtypes.float8_e4m3fn).view(np.uint8)
    return words, np.ascontiguousarray(byte.astype(np.uint8).reshape(k // 512, 16, n))


def unpack_weight(words, scales):
    g, p, n, _ = words.shape
    vals = np.ascontiguousarray(words).view(ml_dtypes.float8_e4m3fn).astype(np.float64) * np.repeat(np.exp2(scales.astype(np.float64) - 127.0), 8, axis=1)[..., None]
    return vals.transpose(0, 1, 3, 2).reshape(g * 512, n)


K, T, D, S, V, N = 512, 512, 4, 512, 128, 128


def setup_inputs():
    n = np.random.standard_normal
    s = mx_kscale(K)[:, None]
    packed = pack_weight(n((K, T)) * s)
    return {
        "x_words": packed[0],
        "x_scales": packed[1],
        "w": (n((D, K, N)) / np.sqrt(D * K) / s[None]).astype(np.float32),
        "gate": np.tile(np.random.uniform(0.2, 1.0, S), (N, 1)).astype(np.float32),
        "offs": striped(np.random.permutation(T)[:S]),
    }


def reference(x_words, x_scales, w, gate, offs):
    idx = unstriped(offs)
    xq = unpack_weight(x_words, x_scales)[:, idx]
    wq = mxq(f64(w), 1, "e4m3")
    y = sum(wq[d].T @ xq[:, d * V:(d + 1) * V] for d in range(D))
    out = np.zeros((N, T))
    out[:, idx] = f64(gate) * np.tile(y, (1, D))
    return out

@@ -1,0 +1,109 @@
+from contextlib import ExitStack
+
+import concourse.mybir as mybir
+
+K, T, D, S, V, N = 512, 512, 4, 512, 128, 128
+FLOPS = 2 * D * K * N * V
+
+F32 = mybir.dt.float32
+BF16 = mybir.dt.bfloat16
+I32 = mybir.dt.int32
+U32 = mybir.dt.uint32
+U16 = mybir.dt.uint16
+U8 = mybir.dt.uint8
+FP8X4 = mybir.dt.float8_e4m3fn_x4
+MULT = mybir.AluOpType.mult
+
+P = 128
+PACK = 4
+LIST_ROWS = 16
+HALF = S // 2
+VEC_COLS = 96
+
+
+def tile_picked_tome_lin_none_sub_p_kernel(tc, x_words, x_scales, w, gate, offs, out):
+    nc = tc.nc
+    with ExitStack() as ctx:
+        pool = ctx.enter_context(tc.tile_pool(name="sbuf", bufs=1))
+        psum = ctx.enter_context(tc.psum_pool(name="psum", bufs=1))
+
+        offsets = pool.tile([P, S // LIST_ROWS], U16, name="offsets")
+        words = pool.tile([P, T], I32, name="words", align_bytes=64)
+        scales = pool.tile([P, T], U8, name="scales", align_bytes=64)
+        w_raw = [pool.tile([P, PACK, N], F32, name=f"w_raw{d}", align_bytes=64) for d in range(D)]
+        gates = pool.tile([P, S], F32, name="gates", align_bytes=64)
+
+        nc.sync.dma_start(offsets[:], offs)
+        scale_rows = x_scales[0].bitcast(I32)
+        for q in range(4):
+            nc.scalar.dma_start(
+                scales[32 * q : 32 * (q + 1), :].bitcast(I32),
+                scale_rows[4 * q : 4 * (q + 1), :].unsqueeze(0).to_broadcast([8, 4, T // 4]),
+            )
+        nc.sync.dma_start(words[:], x_words[0].rearrange("p c r -> p (c r)").bitcast(I32))
+        for d in range(D):
+            nc.sync.dma_start(w_raw[d][:], w[d].rearrange("(p j) m -> p j m", j=PACK))
+        nc.sync.dma_start(gates[:], gate)
+
+        picked_words = pool.tile([P, S], U32, name="picked_words", align_bytes=64)
+        picked_scales = pool.tile([P, S], U8, name="picked_scales", align_bytes=64)
+        for h in range(2):
+            entries = slice(h * HALF, (h + 1) * HALF)
+            cols = offsets[:, h * HALF // LIST_ROWS : (h + 1) * HALF // LIST_ROWS]
+            nc.vector.tensor_copy(picked_scales[:, entries], scales[:].indirect(cols))
+        for h in range(2):
+            entries = slice(h * HALF, (h + 1) * HALF)
+            cols = offsets[:, h * HALF // LIST_ROWS : (h + 1) * HALF // LIST_ROWS]
+            nc.vector.tensor_copy(picked_words[:, entries], words[:].bitcast(U32).indirect(cols))
+
+        grouped = pool.tile([P, D, N, PACK], BF16, name="grouped", align_bytes=64)
+        w_codes = pool.tile([P, D * N], U32, name="w_codes", align_bytes=64)
+        w_scales = pool.tile([P, D * N], U8, name="w_scales", align_bytes=64)
+
+        def interleave(copy, d, lo, hi):
+            copy(
+                grouped[:, d, lo:hi, :].rearrange("p (c i) j -> p c j i", i=4),
+                w_raw[d][:, :, lo:hi].rearrange("p j (c i) -> p c j i", i=4),
+            )
+
+        def quantize(lo, hi):
+            cols = slice(lo * N, hi * N)
+            nc.vector.quantize_mx(
+                out=w_codes[:, cols].bitcast(FP8X4),
+                scales=w_scales[:, cols],
+                in_=grouped[:, lo:hi, :, :].rearrange("p d m j -> p (d m j)"),
+            )
+
+        for d in range(D - 1):
+            interleave(nc.scalar.copy, d, 0, N)
+        quantize(0, 2)
+        interleave(nc.vector.tensor_copy, D - 1, 0, VEC_COLS)
+        interleave(nc.scalar.copy, D - 1, VEC_COLS, N)
+        quantize(2, 3)
+        quantize(3, 4)
+
+        acc = psum.tile([N, V], F32, name="acc")
+        for d in range(D):
+            nc.tensor.matmul_mx(
+                out=acc[:],
+                lhsT=w_codes[:, d * N : (d + 1) * N].bitcast(FP8X4),
+                lhsT_scale=w_scales[:, d * N : (d + 1) * N],
+                rhs=picked_words[:, d * V : (d + 1) * V].bitcast(FP8X4),
+                rhs_scale=picked_scales[:, d * V : (d + 1) * V],
+                start=(d == 0),
+                stop=(d == D - 1),
+            )
+
+        y = pool.tile([N, D, V], F32, name="y", align_bytes=64)
+        nc.scalar.copy(y[:, 0, :], acc[:])
+        nc.scalar.copy(y[:, 1:D, :], acc[:].unsqueeze(1).to_broadcast([N, D - 1, V]))
+        result = pool.tile([N, 2 * T], F32, name="result", align_bytes=64)
+        y_flat = y[:].rearrange("p d v -> p (d v)")
+        for lo, hi in ((0, V), (V, S)):
+            nc.vector.tensor_tensor(
+                result[:].indirect(offsets[:, lo // LIST_ROWS : hi // LIST_ROWS]),
+                y_flat[:, lo:hi],
+                gates[:, lo:hi],
+                MULT,
+            )
+        nc.sync.dma_start(out, result[:, 0:T])

@@ -40,9 +40,10 @@ def tile_picked_tome_lin_none_sub_p_kernel(tc, x_words, x_scales, w, gate, offs,
                 scales[32 * q : 32 * (q + 1), :].bitcast(I32),
                 scale_rows[4 * q : 4 * (q + 1), :].unsqueeze(0).to_broadcast([8, 4, T // 4]),
             )
-        nc.sync.dma_start(words[:], x_words[0].rearrange("p c r -> p (c r)").bitcast(I32))
         for d in range(D):
             nc.sync.dma_start(w_raw[d][:], w[d].rearrange("(p j) m -> p j m", j=PACK))
+            if d == 0:
+                nc.sync.dma_start(words[:], x_words[0].rearrange("p c r -> p (c r)").bitcast(I32))
         nc.sync.dma_start(gates[:], gate)
 
         picked_words = pool.tile([P, S], U32, name="picked_words", align_bytes=64)
@@ -94,16 +95,13 @@ def tile_picked_tome_lin_none_sub_p_kernel(tc, x_words, x_scales, w, gate, offs,
                 stop=(d == D - 1),
             )
 
-        y = pool.tile([N, D, V], F32, name="y", align_bytes=64)
-        nc.scalar.copy(y[:, 0, :], acc[:])
-        nc.scalar.copy(y[:, 1:D, :], acc[:].unsqueeze(1).to_broadcast([N, D - 1, V]))
+        gated = pool.tile([N, S], F32, name="gated", align_bytes=64)
+        nc.vector.tensor_tensor(
+            gated[:].rearrange("p (d v) -> p d v", d=D),
+            acc[:].unsqueeze(1).to_broadcast([N, D, V]),
+            gates[:].rearrange("p (d v) -> p d v", d=D),
+            MULT,
+        )
         result = pool.tile([N, 2 * T], F32, name="result", align_bytes=64)
-        y_flat = y[:].rearrange("p d v -> p (d v)")
-        for lo, hi in ((0, V), (V, S)):
-            nc.vector.tensor_tensor(
-                result[:].indirect(offsets[:, lo // LIST_ROWS : hi // LIST_ROWS]),
-                y_flat[:, lo:hi],
-                gates[:, lo:hi],
-                MULT,
-            )
+        nc.vector.tensor_copy(result[:].indirect(offsets[:]), gated[:])
         nc.sync.dma_start(out, result[:, 0:T])

@@ -33,29 +33,23 @@ def tile_picked_tome_lin_none_sub_p_kernel(tc, x_words, x_scales, w, gate, offs,
         w_raw = [pool.tile([P, PACK, N], F32, name=f"w_raw{d}", align_bytes=64) for d in range(D)]
         gates = pool.tile([P, S], F32, name="gates", align_bytes=64)
 
+        nc.vector.memset(scales[:].bitcast(I32), 0)
         nc.sync.dma_start(offsets[:], offs)
+        nc.sync.dma_start(words[:], x_words[0].rearrange("p c r -> p (c r)").bitcast(I32))
         scale_rows = x_scales[0].bitcast(I32)
         for q in range(4):
-            nc.scalar.dma_start(
-                scales[32 * q : 32 * (q + 1), :].bitcast(I32),
-                scale_rows[4 * q : 4 * (q + 1), :].unsqueeze(0).to_broadcast([8, 4, T // 4]),
-            )
+            queue = nc.sync if q < 2 else nc.scalar
+            queue.dma_start(scales[32 * q : 32 * q + 4, :].bitcast(I32), scale_rows[4 * q : 4 * (q + 1), :])
         for d in range(D):
             nc.sync.dma_start(w_raw[d][:], w[d].rearrange("(p j) m -> p j m", j=PACK))
-            if d == 0:
-                nc.sync.dma_start(words[:], x_words[0].rearrange("p c r -> p (c r)").bitcast(I32))
         nc.sync.dma_start(gates[:], gate)
 
         picked_words = pool.tile([P, S], U32, name="picked_words", align_bytes=64)
         picked_scales = pool.tile([P, S], U8, name="picked_scales", align_bytes=64)
-        for h in range(2):
-            entries = slice(h * HALF, (h + 1) * HALF)
-            cols = offsets[:, h * HALF // LIST_ROWS : (h + 1) * HALF // LIST_ROWS]
-            nc.vector.tensor_copy(picked_scales[:, entries], scales[:].indirect(cols))
-        for h in range(2):
-            entries = slice(h * HALF, (h + 1) * HALF)
-            cols = offsets[:, h * HALF // LIST_ROWS : (h + 1) * HALF // LIST_ROWS]
-            nc.vector.tensor_copy(picked_words[:, entries], words[:].bitcast(U32).indirect(cols))
+
+        def gather(picked, window, lo, hi):
+            cols = offsets[:, lo // LIST_ROWS : hi // LIST_ROWS]
+            nc.vector.tensor_copy(picked[:, lo:hi], window.indirect(cols))
 
         grouped = pool.tile([P, D, N, PACK], BF16, name="grouped", align_bytes=64)
         w_codes = pool.tile([P, D * N], U32, name="w_codes", align_bytes=64)
@@ -77,9 +71,14 @@ def tile_picked_tome_lin_none_sub_p_kernel(tc, x_words, x_scales, w, gate, offs,
 
         for d in range(D - 1):
             interleave(nc.scalar.copy, d, 0, N)
-        quantize(0, 2)
-        interleave(nc.vector.tensor_copy, D - 1, 0, VEC_COLS)
         interleave(nc.scalar.copy, D - 1, VEC_COLS, N)
+        gather(picked_words, words[:].bitcast(U32), 0, HALF)
+        gather(picked_words, words[:].bitcast(U32), HALF, S)
+        quantize(0, 1)
+        quantize(1, 2)
+        gather(picked_scales, scales[:], 0, HALF)
+        gather(picked_scales, scales[:], HALF, S)
+        interleave(nc.vector.tensor_copy, D - 1, 0, VEC_COLS)
         quantize(2, 3)
         quantize(3, 4)
 

@@ -18,7 +18,7 @@ P = 128
 PACK = 4
 LIST_ROWS = 16
 HALF = S // 2
-VEC_COLS = 96
+VEC_COLS = 48
 
 
 def tile_picked_tome_lin_none_sub_p_kernel(tc, x_words, x_scales, w, gate, offs, out):
@@ -28,18 +28,18 @@ def tile_picked_tome_lin_none_sub_p_kernel(tc, x_words, x_scales, w, gate, offs,
         psum = ctx.enter_context(tc.psum_pool(name="psum", bufs=1))
 
         offsets = pool.tile([P, S // LIST_ROWS], U16, name="offsets")
-        words = pool.tile([P, T], I32, name="words", align_bytes=64)
-        scales = pool.tile([P, T], U8, name="scales", align_bytes=64)
+        words = pool.tile([P, 2 * T], I32, name="words", align_bytes=64)
+        scales = pool.tile([P, 2 * T], U8, name="scales", align_bytes=64)
         w_raw = [pool.tile([P, PACK, N], F32, name=f"w_raw{d}", align_bytes=64) for d in range(D)]
         gates = pool.tile([P, S], F32, name="gates", align_bytes=64)
 
-        nc.vector.memset(scales[:].bitcast(I32), 0)
+        nc.vector.memset(scales[:, 0:T].bitcast(I32), 0)
         nc.sync.dma_start(offsets[:], offs)
-        nc.sync.dma_start(words[:], x_words[0].rearrange("p c r -> p (c r)").bitcast(I32))
+        nc.sync.dma_start(words[:, 0:T], x_words[0].rearrange("p c r -> p (c r)").bitcast(I32))
         scale_rows = x_scales[0].bitcast(I32)
         for q in range(4):
             queue = nc.sync if q < 2 else nc.scalar
-            queue.dma_start(scales[32 * q : 32 * q + 4, :].bitcast(I32), scale_rows[4 * q : 4 * (q + 1), :])
+            queue.dma_start(scales[32 * q : 32 * q + 4, 0:T].bitcast(I32), scale_rows[4 * q : 4 * (q + 1), :])
         for d in range(D):
             nc.sync.dma_start(w_raw[d][:], w[d].rearrange("(p j) m -> p j m", j=PACK))
         nc.sync.dma_start(gates[:], gate)
@@ -72,12 +72,10 @@ def tile_picked_tome_lin_none_sub_p_kernel(tc, x_words, x_scales, w, gate, offs,
         for d in range(D - 1):
             interleave(nc.scalar.copy, d, 0, N)
         interleave(nc.scalar.copy, D - 1, VEC_COLS, N)
-        gather(picked_words, words[:].bitcast(U32), 0, HALF)
-        gather(picked_words, words[:].bitcast(U32), HALF, S)
+        gather(picked_words, words[:].bitcast(U32), 0, S)
         quantize(0, 1)
         quantize(1, 2)
-        gather(picked_scales, scales[:], 0, HALF)
-        gather(picked_scales, scales[:], HALF, S)
+        gather(picked_scales, scales[:], 0, S)
         interleave(nc.vector.tensor_copy, D - 1, 0, VEC_COLS)
         quantize(2, 3)
         quantize(3, 4)

@@ -92,13 +92,11 @@ def tile_picked_tome_lin_none_sub_p_kernel(tc, x_words, x_scales, w, gate, offs,
                 stop=(d == D - 1),
             )
 
-        gated = pool.tile([N, S], F32, name="gated", align_bytes=64)
-        nc.vector.tensor_tensor(
-            gated[:].rearrange("p (d v) -> p d v", d=D),
+        repeated = pool.tile([N, S], F32, name="repeated", align_bytes=64)
+        nc.scalar.copy(
+            repeated[:].rearrange("p (d v) -> p d v", d=D),
             acc[:].unsqueeze(1).to_broadcast([N, D, V]),
-            gates[:].rearrange("p (d v) -> p d v", d=D),
-            MULT,
         )
         result = pool.tile([N, 2 * T], F32, name="result", align_bytes=64)
-        nc.vector.tensor_copy(result[:].indirect(offsets[:]), gated[:])
+        nc.vector.tensor_tensor(result[:].indirect(offsets[:]), repeated[:], gates[:], MULT)
         nc.sync.dma_start(out, result[:, 0:T])

@@ -18,7 +18,7 @@ P = 128
 PACK = 4
 LIST_ROWS = 16
 HALF = S // 2
-VEC_COLS = 48
+VEC_COLS = 64
 
 
 def tile_picked_tome_lin_none_sub_p_kernel(tc, x_words, x_scales, w, gate, offs, out):

@@ -30,8 +30,7 @@ def tile_picked_tome_lin_none_sub_p_kernel(tc, x_words, x_scales, w, gate, offs,
         offsets = pool.tile([P, S // LIST_ROWS], U16, name="offsets")
         words = pool.tile([P, 2 * T], I32, name="words", align_bytes=64)
         scales = pool.tile([P, 2 * T], U8, name="scales", align_bytes=64)
-        w_raw = [pool.tile([P, PACK, N], F32, name=f"w_raw{d}", align_bytes=64) for d in range(D)]
-        gates = pool.tile([P, S], F32, name="gates", align_bytes=64)
+        w_raw = [pool.tile([P, PACK, N], F32, name=f"w_raw{d}", tag=f"slot{d}", align_bytes=64) for d in range(D)]
 
         nc.vector.memset(scales[:, 0:T].bitcast(I32), 0)
         nc.sync.dma_start(offsets[:], offs)
@@ -42,7 +41,6 @@ def tile_picked_tome_lin_none_sub_p_kernel(tc, x_words, x_scales, w, gate, offs,
             queue.dma_start(scales[32 * q : 32 * q + 4, 0:T].bitcast(I32), scale_rows[4 * q : 4 * (q + 1), :])
         for d in range(D):
             nc.sync.dma_start(w_raw[d][:], w[d].rearrange("(p j) m -> p j m", j=PACK))
-        nc.sync.dma_start(gates[:], gate)
 
         picked_words = pool.tile([P, S], U32, name="picked_words", align_bytes=64)
         picked_scales = pool.tile([P, S], U8, name="picked_scales", align_bytes=64)
@@ -72,6 +70,8 @@ def tile_picked_tome_lin_none_sub_p_kernel(tc, x_words, x_scales, w, gate, offs,
         for d in range(D - 1):
             interleave(nc.scalar.copy, d, 0, N)
         interleave(nc.scalar.copy, D - 1, VEC_COLS, N)
+        gates = pool.tile([P, S], F32, name="gates", tag="slot0", align_bytes=64)
+        nc.sync.dma_start(gates[:], gate)
         gather(picked_words, words[:].bitcast(U32), 0, S)
         quantize(0, 1)
         quantize(1, 2)

@@ -37,8 +37,7 @@ def tile_picked_tome_lin_none_sub_p_kernel(tc, x_words, x_scales, w, gate, offs,
         nc.sync.dma_start(words[:, 0:T], x_words[0].rearrange("p c r -> p (c r)").bitcast(I32))
         scale_rows = x_scales[0].bitcast(I32)
         for q in range(4):
-            queue = nc.sync if q < 2 else nc.scalar
-            queue.dma_start(scales[32 * q : 32 * q + 4, 0:T].bitcast(I32), scale_rows[4 * q : 4 * (q + 1), :])
+            nc.scalar.dma_start(scales[32 * q : 32 * q + 4, 0:T].bitcast(I32), scale_rows[4 * q : 4 * (q + 1), :])
         for d in range(D):
             nc.sync.dma_start(w_raw[d][:], w[d].rearrange("(p j) m -> p j m", j=PACK))
 

@@ -33,10 +33,13 @@ def tile_picked_tome_lin_none_sub_p_kernel(tc, x_words, x_scales, w, gate, offs,
         w_raw = [pool.tile([P, PACK, N], F32, name=f"w_raw{d}", tag=f"slot{d}", align_bytes=64) for d in range(D)]
 
         nc.vector.memset(scales[:, 0:T].bitcast(I32), 0)
-        nc.sync.dma_start(offsets[:], offs)
-        nc.sync.dma_start(words[:, 0:T], x_words[0].rearrange("p c r -> p (c r)").bitcast(I32))
         scale_rows = x_scales[0].bitcast(I32)
-        for q in range(4):
+        staged = pool.tile([4, T // 4], I32, name="staged", align_bytes=64)
+        nc.scalar.dma_start(staged[:], scale_rows[0:4, :])
+        nc.gpsimd.tensor_copy(scales[0:4, 0:T].bitcast(I32), staged[:])
+        nc.sync.dma_start(words[:, 0:T], x_words[0].rearrange("p c r -> p (c r)").bitcast(I32))
+        nc.sync.dma_start(offsets[:], offs)
+        for q in range(1, 4):
             nc.scalar.dma_start(scales[32 * q : 32 * q + 4, 0:T].bitcast(I32), scale_rows[4 * q : 4 * (q + 1), :])
         for d in range(D):
             nc.sync.dma_start(w_raw[d][:], w[d].rearrange("(p j) m -> p j m", j=PACK))

@@ -18,7 +18,7 @@ P = 128
 PACK = 4
 LIST_ROWS = 16
 HALF = S // 2
-VEC_COLS = 64
+VEC_COLS = 56
 
 
 def tile_picked_tome_lin_none_sub_p_kernel(tc, x_words, x_scales, w, gate, offs, out):
@@ -39,10 +39,15 @@ def tile_picked_tome_lin_none_sub_p_kernel(tc, x_words, x_scales, w, gate, offs,
         nc.gpsimd.tensor_copy(scales[0:4, 0:T].bitcast(I32), staged[:])
         nc.sync.dma_start(words[:, 0:T], x_words[0].rearrange("p c r -> p (c r)").bitcast(I32))
         nc.sync.dma_start(offsets[:], offs)
-        for q in range(1, 4):
-            nc.scalar.dma_start(scales[32 * q : 32 * q + 4, 0:T].bitcast(I32), scale_rows[4 * q : 4 * (q + 1), :])
-        for d in range(D):
+
+        def load_w(d):
             nc.sync.dma_start(w_raw[d][:], w[d].rearrange("(p j) m -> p j m", j=PACK))
+
+        load_w(0)
+        for q in range(1, 4):
+            nc.sync.dma_start(scales[32 * q : 32 * q + 4, 0:T].bitcast(I32), scale_rows[4 * q : 4 * (q + 1), :])
+        for d in range(1, D):
+            load_w(d)
 
         picked_words = pool.tile([P, S], U32, name="picked_words", align_bytes=64)
         picked_scales = pool.tile([P, S], U8, name="picked_scales", align_bytes=64)
@@ -52,7 +57,7 @@ def tile_picked_tome_lin_none_sub_p_kernel(tc, x_words, x_scales, w, gate, offs,
             nc.vector.tensor_copy(picked[:, lo:hi], window.indirect(cols))
 
         grouped = pool.tile([P, D, N, PACK], BF16, name="grouped", align_bytes=64)
-        w_codes = pool.tile([P, D * N], U32, name="w_codes", align_bytes=64)
+        w_codes = {}
         w_scales = pool.tile([P, D * N], U8, name="w_scales", align_bytes=64)
 
         def interleave(copy, d, lo, hi):
@@ -61,12 +66,13 @@ def tile_picked_tome_lin_none_sub_p_kernel(tc, x_words, x_scales, w, gate, offs,
                 w_raw[d][:, :, lo:hi].rearrange("p j (c i) -> p c j i", i=4),
             )
 
-        def quantize(lo, hi):
-            cols = slice(lo * N, hi * N)
+        def quantize(d):
+            tag = "slot2" if d == 1 else f"w_codes{d}"
+            w_codes[d] = pool.tile([P, N], U32, name=f"w_codes{d}", tag=tag, align_bytes=64)
             nc.vector.quantize_mx(
-                out=w_codes[:, cols].bitcast(FP8X4),
-                scales=w_scales[:, cols],
-                in_=grouped[:, lo:hi, :, :].rearrange("p d m j -> p (d m j)"),
+                out=w_codes[d][:].bitcast(FP8X4),
+                scales=w_scales[:, d * N : (d + 1) * N],
+                in_=grouped[:, d, :, :].rearrange("p m j -> p (m j)"),
             )
 
         for d in range(D - 1):
@@ -75,18 +81,17 @@ def tile_picked_tome_lin_none_sub_p_kernel(tc, x_words, x_scales, w, gate, offs,
         gates = pool.tile([P, S], F32, name="gates", tag="slot0", align_bytes=64)
         nc.sync.dma_start(gates[:], gate)
         gather(picked_words, words[:].bitcast(U32), 0, S)
-        quantize(0, 1)
-        quantize(1, 2)
         gather(picked_scales, scales[:], 0, S)
+        quantize(0)
         interleave(nc.vector.tensor_copy, D - 1, 0, VEC_COLS)
-        quantize(2, 3)
-        quantize(3, 4)
+        for d in range(1, D):
+            quantize(d)
 
         acc = psum.tile([N, V], F32, name="acc")
         for d in range(D):
             nc.tensor.matmul_mx(
                 out=acc[:],
-                lhsT=w_codes[:, d * N : (d + 1) * N].bitcast(FP8X4),
+                lhsT=w_codes[d][:].bitcast(FP8X4),
                 lhsT_scale=w_scales[:, d * N : (d + 1) * N],
                 rhs=picked_words[:, d * V : (d + 1) * V].bitcast(FP8X4),
                 rhs_scale=picked_scales[:, d * V : (d + 1) * V],

@@ -18,7 +18,7 @@ P = 128
 PACK = 4
 LIST_ROWS = 16
 HALF = S // 2
-VEC_COLS = 56
+VEC_COLS = 64
 
 
 def tile_picked_tome_lin_none_sub_p_kernel(tc, x_words, x_scales, w, gate, offs, out):
@@ -66,13 +66,14 @@ def tile_picked_tome_lin_none_sub_p_kernel(tc, x_words, x_scales, w, gate, offs,
                 w_raw[d][:, :, lo:hi].rearrange("p j (c i) -> p c j i", i=4),
             )
 
-        def quantize(d):
-            tag = "slot2" if d == 1 else f"w_codes{d}"
-            w_codes[d] = pool.tile([P, N], U32, name=f"w_codes{d}", tag=tag, align_bytes=64)
+        def quantize(d, lo, hi):
+            if d not in w_codes:
+                tag = "slot2" if d == D - 1 else f"w_codes{d}"
+                w_codes[d] = pool.tile([P, N], U32, name=f"w_codes{d}", tag=tag, align_bytes=64)
             nc.vector.quantize_mx(
-                out=w_codes[d][:].bitcast(FP8X4),
-                scales=w_scales[:, d * N : (d + 1) * N],
-                in_=grouped[:, d, :, :].rearrange("p m j -> p (m j)"),
+                out=w_codes[d][:, lo:hi].bitcast(FP8X4),
+                scales=w_scales[:, d * N + lo : d * N + hi],
+                in_=grouped[:, d, lo:hi, :].rearrange("p m j -> p (m j)"),
             )
 
         for d in range(D - 1):
@@ -82,10 +83,12 @@ def tile_picked_tome_lin_none_sub_p_kernel(tc, x_words, x_scales, w, gate, offs,
         nc.sync.dma_start(gates[:], gate)
         gather(picked_words, words[:].bitcast(U32), 0, S)
         gather(picked_scales, scales[:], 0, S)
-        quantize(0)
+        quantize(0, 0, N)
+        quantize(1, 0, N)
         interleave(nc.vector.tensor_copy, D - 1, 0, VEC_COLS)
-        for d in range(1, D):
-            quantize(d)
+        quantize(2, 0, N)
+        quantize(3, 0, VEC_COLS)
+        quantize(3, VEC_COLS, N)
 
         acc = psum.tile([N, V], F32, name="acc")
         for d in range(D):

@@ -34,11 +34,16 @@ def tile_picked_tome_lin_none_sub_p_kernel(tc, x_words, x_scales, w, gate, offs,
 
         nc.vector.memset(scales[:, 0:T].bitcast(I32), 0)
         scale_rows = x_scales[0].bitcast(I32)
-        staged = pool.tile([4, T // 4], I32, name="staged", align_bytes=64)
-        nc.scalar.dma_start(staged[:], scale_rows[0:4, :])
-        nc.gpsimd.tensor_copy(scales[0:4, 0:T].bitcast(I32), staged[:])
-        nc.sync.dma_start(words[:, 0:T], x_words[0].rearrange("p c r -> p (c r)").bitcast(I32))
+        early_scales = pool.tile([P, 2 * T], U8, name="early_scales", align_bytes=64)
+        nc.vector.memset(early_scales[:, 0:T].bitcast(I32), 0)
+        placed_scales = pool.tile([P, V], U8, name="placed_scales", align_bytes=64)
+        nc.vector.memset(placed_scales[:].bitcast(I32), 0)
+        staged = pool.tile([16, T // 4], I32, name="staged", align_bytes=64)
+        nc.scalar.dma_start(staged[:], scale_rows)
+        nc.vector.tensor_copy(early_scales[0:16, 0:T].bitcast(I32), staged[:])
+        nc.vector.tensor_copy(scales[0:4, 0:T].bitcast(I32), staged[0:4, :])
         nc.sync.dma_start(offsets[:], offs)
+        nc.sync.dma_start(words[:, 0:T], x_words[0].rearrange("p c r -> p (c r)").bitcast(I32))
 
         def load_w(d):
             nc.sync.dma_start(w_raw[d][:], w[d].rearrange("(p j) m -> p j m", j=PACK))
@@ -50,11 +55,12 @@ def tile_picked_tome_lin_none_sub_p_kernel(tc, x_words, x_scales, w, gate, offs,
             load_w(d)
 
         picked_words = pool.tile([P, S], U32, name="picked_words", align_bytes=64)
-        picked_scales = pool.tile([P, S], U8, name="picked_scales", align_bytes=64)
+        picked_scales = pool.tile([P, S - V], U8, name="picked_scales", align_bytes=64)
+        picked_early = pool.tile([P, V], U8, name="picked_early", align_bytes=64)
 
         def gather(picked, window, lo, hi):
             cols = offsets[:, lo // LIST_ROWS : hi // LIST_ROWS]
-            nc.vector.tensor_copy(picked[:, lo:hi], window.indirect(cols))
+            nc.vector.tensor_copy(picked[:], window.indirect(cols))
 
         grouped = pool.tile([P, D, N, PACK], BF16, name="grouped", align_bytes=64)
         w_codes = {}
@@ -79,10 +85,15 @@ def tile_picked_tome_lin_none_sub_p_kernel(tc, x_words, x_scales, w, gate, offs,
         for d in range(D - 1):
             interleave(nc.scalar.copy, d, 0, N)
         interleave(nc.scalar.copy, D - 1, VEC_COLS, N)
+        gather(picked_early, early_scales[:], S - V, S)
+        for q in range(4):
+            nc.sync.dma_start(
+                placed_scales[32 * q : 32 * q + 4, :].bitcast(I32), picked_early[4 * q : 4 * q + 4, :].bitcast(I32)
+            )
         gates = pool.tile([P, S], F32, name="gates", tag="slot0", align_bytes=64)
         nc.sync.dma_start(gates[:], gate)
         gather(picked_words, words[:].bitcast(U32), 0, S)
-        gather(picked_scales, scales[:], 0, S)
+        gather(picked_scales, scales[:], 0, S - V)
         quantize(0, 0, N)
         quantize(1, 0, N)
         interleave(nc.vector.tensor_copy, D - 1, 0, VEC_COLS)
@@ -97,7 +108,7 @@ def tile_picked_tome_lin_none_sub_p_kernel(tc, x_words, x_scales, w, gate, offs,
                 lhsT=w_codes[d][:].bitcast(FP8X4),
                 lhsT_scale=w_scales[:, d * N : (d + 1) * N],
                 rhs=picked_words[:, d * V : (d + 1) * V].bitcast(FP8X4),
-                rhs_scale=picked_scales[:, d * V : (d + 1) * V],
+                rhs_scale=placed_scales[:] if d == D - 1 else picked_scales[:, d * V : (d + 1) * V],
                 start=(d == 0),
                 stop=(d == D - 1),
             )

@@ -36,7 +36,7 @@ def tile_picked_tome_lin_none_sub_p_kernel(tc, x_words, x_scales, w, gate, offs,
         scale_rows = x_scales[0].bitcast(I32)
         early_scales = pool.tile([P, 2 * T], U8, name="early_scales", align_bytes=64)
         nc.vector.memset(early_scales[:, 0:T].bitcast(I32), 0)
-        placed_scales = pool.tile([P, V], U8, name="placed_scales", align_bytes=64)
+        placed_scales = pool.tile([P, HALF], U8, name="placed_scales", align_bytes=64)
         nc.vector.memset(placed_scales[:].bitcast(I32), 0)
         staged = pool.tile([16, T // 4], I32, name="staged", align_bytes=64)
         nc.scalar.dma_start(staged[:], scale_rows)
@@ -55,8 +55,8 @@ def tile_picked_tome_lin_none_sub_p_kernel(tc, x_words, x_scales, w, gate, offs,
             load_w(d)
 
         picked_words = pool.tile([P, S], U32, name="picked_words", align_bytes=64)
-        picked_scales = pool.tile([P, S - V], U8, name="picked_scales", align_bytes=64)
-        picked_early = pool.tile([P, V], U8, name="picked_early", align_bytes=64)
+        picked_scales = pool.tile([P, HALF], U8, name="picked_scales", align_bytes=64)
+        picked_early = pool.tile([P, HALF], U8, name="picked_early", align_bytes=64)
 
         def gather(picked, window, lo, hi):
             cols = offsets[:, lo // LIST_ROWS : hi // LIST_ROWS]
@@ -85,7 +85,7 @@ def tile_picked_tome_lin_none_sub_p_kernel(tc, x_words, x_scales, w, gate, offs,
         for d in range(D - 1):
             interleave(nc.scalar.copy, d, 0, N)
         interleave(nc.scalar.copy, D - 1, VEC_COLS, N)
-        gather(picked_early, early_scales[:], S - V, S)
+        gather(picked_early, early_scales[:], HALF, S)
         for q in range(4):
             nc.sync.dma_start(
                 placed_scales[32 * q : 32 * q + 4, :].bitcast(I32), picked_early[4 * q : 4 * q + 4, :].bitcast(I32)
@@ -93,7 +93,7 @@ def tile_picked_tome_lin_none_sub_p_kernel(tc, x_words, x_scales, w, gate, offs,
         gates = pool.tile([P, S], F32, name="gates", tag="slot0", align_bytes=64)
         nc.sync.dma_start(gates[:], gate)
         gather(picked_words, words[:].bitcast(U32), 0, S)
-        gather(picked_scales, scales[:], 0, S - V)
+        gather(picked_scales, scales[:], 0, HALF)
         quantize(0, 0, N)
         quantize(1, 0, N)
         interleave(nc.vector.tensor_copy, D - 1, 0, VEC_COLS)
@@ -108,7 +108,7 @@ def tile_picked_tome_lin_none_sub_p_kernel(tc, x_words, x_scales, w, gate, offs,
                 lhsT=w_codes[d][:].bitcast(FP8X4),
                 lhsT_scale=w_scales[:, d * N : (d + 1) * N],
                 rhs=picked_words[:, d * V : (d + 1) * V].bitcast(FP8X4),
-                rhs_scale=placed_scales[:] if d == D - 1 else picked_scales[:, d * V : (d + 1) * V],
+                rhs_scale=(picked_scales, placed_scales)[d // 2][:, d % 2 * V : (d % 2 + 1) * V],
                 start=(d == 0),
                 stop=(d == D - 1),
             )

@@ -13,6 +13,8 @@ U16 = mybir.dt.uint16
 U8 = mybir.dt.uint8
 FP8X4 = mybir.dt.float8_e4m3fn_x4
 MULT = mybir.AluOpType.mult
+ADD = mybir.AluOpType.add
+COPY = mybir.ActivationFunctionType.Copy
 
 P = 128
 PACK = 4
@@ -90,7 +92,7 @@ def tile_picked_tome_lin_none_sub_p_kernel(tc, x_words, x_scales, w, gate, offs,
             nc.sync.dma_start(
                 placed_scales[32 * q : 32 * q + 4, :].bitcast(I32), picked_early[4 * q : 4 * q + 4, :].bitcast(I32)
             )
-        gates = pool.tile([P, S], F32, name="gates", tag="slot0", align_bytes=64)
+        gates = pool.tile([P, S], F32, name="gates", align_bytes=64)
         nc.sync.dma_start(gates[:], gate)
         gather(picked_words, words[:].bitcast(U32), 0, S)
         gather(picked_scales, scales[:], 0, HALF)
@@ -113,11 +115,21 @@ def tile_picked_tome_lin_none_sub_p_kernel(tc, x_words, x_scales, w, gate, offs,
                 stop=(d == D - 1),
             )
 
-        repeated = pool.tile([N, S], F32, name="repeated", align_bytes=64)
-        nc.scalar.copy(
-            repeated[:].rearrange("p (d v) -> p d v", d=D),
-            acc[:].unsqueeze(1).to_broadcast([N, D, V]),
-        )
-        result = pool.tile([N, 2 * T], F32, name="result", align_bytes=64)
-        nc.vector.tensor_tensor(result[:].indirect(offsets[:]), repeated[:], gates[:], MULT)
-        nc.sync.dma_start(out, result[:, 0:T])
+        gated = pool.tile([N, S], F32, name="gated", align_bytes=64)
+        by_scalar = pool.tile([N, T], F32, name="by_scalar", align_bytes=64)
+        by_vector = pool.tile([N, T], F32, name="by_vector", align_bytes=64)
+        nc.gpsimd.memset(by_scalar[:], 0.0)
+        nc.gpsimd.memset(by_vector[:], 0.0)
+        for lo, hi in ((0, HALF), (HALF, S)):
+            nc.vector.tensor_tensor(
+                gated[:, lo:hi].rearrange("p (d v) -> p d v", v=V),
+                acc[:].unsqueeze(1).to_broadcast([N, (hi - lo) // V, V]),
+                gates[:, lo:hi].rearrange("p (d v) -> p d v", v=V),
+                MULT,
+            )
+        nc.scalar.activation(by_scalar[:].indirect(offsets[:, 0 : HALF // LIST_ROWS]), gated[:, 0:HALF], COPY)
+        nc.vector.tensor_copy(by_vector[:].indirect(offsets[:, HALF // LIST_ROWS :]), gated[:, HALF:S])
+        result = pool.tile([N, T], F32, name="result", align_bytes=64)
+        for lo, hi in ((0, T // 2), (T // 2, T)):
+            nc.vector.tensor_tensor(result[:, lo:hi], by_scalar[:, lo:hi], by_vector[:, lo:hi], ADD)
+            nc.sync.dma_start(out[:, lo:hi], result[:, lo:hi])

@@ -118,8 +118,8 @@ def tile_picked_tome_lin_none_sub_p_kernel(tc, x_words, x_scales, w, gate, offs,
         gated = pool.tile([N, S], F32, name="gated", align_bytes=64)
         by_scalar = pool.tile([N, T], F32, name="by_scalar", align_bytes=64)
         by_vector = pool.tile([N, T], F32, name="by_vector", align_bytes=64)
-        nc.gpsimd.memset(by_scalar[:], 0.0)
-        nc.gpsimd.memset(by_vector[:], 0.0)
+        nc.vector.memset(by_scalar[:], 0.0)
+        nc.vector.memset(by_vector[:], 0.0)
         for lo, hi in ((0, HALF), (HALF, S)):
             nc.vector.tensor_tensor(
                 gated[:, lo:hi].rearrange("p (d v) -> p d v", v=V),

@@ -55,6 +55,8 @@ def tile_picked_tome_lin_none_sub_p_kernel(tc, x_words, x_scales, w, gate, offs,
             nc.sync.dma_start(scales[32 * q : 32 * q + 4, 0:T].bitcast(I32), scale_rows[4 * q : 4 * (q + 1), :])
         for d in range(1, D):
             load_w(d)
+        gates = [pool.tile([P, HALF], F32, name=f"gates{h}", align_bytes=64) for h in range(2)]
+        nc.sync.dma_start(gates[0][:], gate[:, 0:HALF])
 
         picked_words = pool.tile([P, S], U32, name="picked_words", align_bytes=64)
         picked_scales = pool.tile([P, HALF], U8, name="picked_scales", align_bytes=64)
@@ -92,8 +94,7 @@ def tile_picked_tome_lin_none_sub_p_kernel(tc, x_words, x_scales, w, gate, offs,
             nc.sync.dma_start(
                 placed_scales[32 * q : 32 * q + 4, :].bitcast(I32), picked_early[4 * q : 4 * q + 4, :].bitcast(I32)
             )
-        gates = pool.tile([P, S], F32, name="gates", align_bytes=64)
-        nc.sync.dma_start(gates[:], gate)
+        nc.sync.dma_start(gates[1][:], gate[:, HALF:S])
         gather(picked_words, words[:].bitcast(U32), 0, S)
         gather(picked_scales, scales[:], 0, HALF)
         quantize(0, 0, N)
@@ -120,15 +121,15 @@ def tile_picked_tome_lin_none_sub_p_kernel(tc, x_words, x_scales, w, gate, offs,
         by_vector = pool.tile([N, T], F32, name="by_vector", align_bytes=64)
         nc.vector.memset(by_scalar[:], 0.0)
         nc.vector.memset(by_vector[:], 0.0)
-        for lo, hi in ((0, HALF), (HALF, S)):
+        for h, (lo, hi) in enumerate(((0, HALF), (HALF, S))):
             nc.vector.tensor_tensor(
                 gated[:, lo:hi].rearrange("p (d v) -> p d v", v=V),
                 acc[:].unsqueeze(1).to_broadcast([N, (hi - lo) // V, V]),
-                gates[:, lo:hi].rearrange("p (d v) -> p d v", v=V),
+                gates[h][:].rearrange("p (d v) -> p d v", v=V),
                 MULT,
             )
-        nc.scalar.activation(by_scalar[:].indirect(offsets[:, 0 : HALF // LIST_ROWS]), gated[:, 0:HALF], COPY)
-        nc.vector.tensor_copy(by_vector[:].indirect(offsets[:, HALF // LIST_ROWS :]), gated[:, HALF:S])
+        nc.vector.tensor_copy(by_vector[:].indirect(offsets[:, 0 : HALF // LIST_ROWS]), gated[:, 0:HALF])
+        nc.scalar.activation(by_scalar[:].indirect(offsets[:, HALF // LIST_ROWS :]), gated[:, HALF:S], COPY)
         result = pool.tile([N, T], F32, name="result", align_bytes=64)
         for lo, hi in ((0, T // 2), (T // 2, T)):
             nc.vector.tensor_tensor(result[:, lo:hi], by_scalar[:, lo:hi], by_vector[:, lo:hi], ADD)

@@ -131,6 +131,6 @@ def tile_picked_tome_lin_none_sub_p_kernel(tc, x_words, x_scales, w, gate, offs,
         nc.vector.tensor_copy(by_vector[:].indirect(offsets[:, 0 : HALF // LIST_ROWS]), gated[:, 0:HALF])
         nc.scalar.activation(by_scalar[:].indirect(offsets[:, HALF // LIST_ROWS :]), gated[:, HALF:S], COPY)
         result = pool.tile([N, T], F32, name="result", align_bytes=64)
-        for lo, hi in ((0, T // 2), (T // 2, T)):
+        for lo, hi in ((0, 128), (128, 320), (320, T)):
             nc.vector.tensor_tensor(result[:, lo:hi], by_scalar[:, lo:hi], by_vector[:, lo:hi], ADD)
             nc.sync.dma_start(out[:, lo:hi], result[:, lo:hi])

@@ -116,21 +116,23 @@ def tile_picked_tome_lin_none_sub_p_kernel(tc, x_words, x_scales, w, gate, offs,
                 stop=(d == D - 1),
             )
 
-        gated = pool.tile([N, S], F32, name="gated", align_bytes=64)
         by_scalar = pool.tile([N, T], F32, name="by_scalar", align_bytes=64)
         by_vector = pool.tile([N, T], F32, name="by_vector", align_bytes=64)
-        nc.vector.memset(by_scalar[:], 0.0)
-        nc.vector.memset(by_vector[:], 0.0)
-        for h, (lo, hi) in enumerate(((0, HALF), (HALF, S))):
-            nc.vector.tensor_tensor(
-                gated[:, lo:hi].rearrange("p (d v) -> p d v", v=V),
-                acc[:].unsqueeze(1).to_broadcast([N, (hi - lo) // V, V]),
-                gates[h][:].rearrange("p (d v) -> p d v", v=V),
-                MULT,
-            )
-        nc.vector.tensor_copy(by_vector[:].indirect(offsets[:, 0 : HALF // LIST_ROWS]), gated[:, 0:HALF])
-        nc.scalar.activation(by_scalar[:].indirect(offsets[:, HALF // LIST_ROWS :]), gated[:, HALF:S], COPY)
+        nc.vector.memset(by_scalar[:], 1.0)
+        nc.vector.memset(by_vector[:], 1.0)
+
+        def entries(lo, hi):
+            return offsets[:, lo // LIST_ROWS : hi // LIST_ROWS]
+
+        nc.scalar.activation(by_vector[:].indirect(entries(V, HALF)), gates[0][:, V:HALF], COPY)
+        sources = pool.tile([N, 3 * V], F32, name="sources", align_bytes=64)
+        nc.vector.tensor_copy(
+            sources[:, V : 3 * V].rearrange("p (d v) -> p d v", v=V), acc[:].unsqueeze(1).to_broadcast([N, 2, V])
+        )
+        nc.vector.tensor_tensor(sources[:, 0:V], acc[:], gates[0][:, 0:V], MULT)
+        nc.scalar.activation(by_scalar[:].indirect(entries(0, HALF)), sources[:, 0:HALF], COPY)
+        nc.vector.tensor_tensor(by_vector[:].indirect(entries(HALF, S)), sources[:, V : 3 * V], gates[1][:], MULT)
         result = pool.tile([N, T], F32, name="result", align_bytes=64)
         for lo, hi in ((0, 128), (128, 320), (320, T)):
-            nc.vector.tensor_tensor(result[:, lo:hi], by_scalar[:, lo:hi], by_vector[:, lo:hi], ADD)
+            nc.vector.tensor_tensor(result[:, lo:hi], by_scalar[:, lo:hi], by_vector[:, lo:hi], MULT)
             nc.sync.dma_start(out[:, lo:hi], result[:, lo:hi])

@@ -55,8 +55,9 @@ def tile_picked_tome_lin_none_sub_p_kernel(tc, x_words, x_scales, w, gate, offs,
             nc.sync.dma_start(scales[32 * q : 32 * q + 4, 0:T].bitcast(I32), scale_rows[4 * q : 4 * (q + 1), :])
         for d in range(1, D):
             load_w(d)
-        gates = [pool.tile([P, HALF], F32, name=f"gates{h}", align_bytes=64) for h in range(2)]
-        nc.sync.dma_start(gates[0][:], gate[:, 0:HALF])
+        early_gates = pool.tile([P, V], F32, name="early_gates", align_bytes=64)
+        late_gates = pool.tile([P, S - V], F32, name="late_gates", align_bytes=64)
+        nc.sync.dma_start(early_gates[:], gate[:, 0:V])
 
         picked_words = pool.tile([P, S], U32, name="picked_words", align_bytes=64)
         picked_scales = pool.tile([P, HALF], U8, name="picked_scales", align_bytes=64)
@@ -94,7 +95,7 @@ def tile_picked_tome_lin_none_sub_p_kernel(tc, x_words, x_scales, w, gate, offs,
             nc.sync.dma_start(
                 placed_scales[32 * q : 32 * q + 4, :].bitcast(I32), picked_early[4 * q : 4 * q + 4, :].bitcast(I32)
             )
-        nc.sync.dma_start(gates[1][:], gate[:, HALF:S])
+        nc.sync.dma_start(late_gates[:], gate[:, V:S])
         gather(picked_words, words[:].bitcast(U32), 0, S)
         gather(picked_scales, scales[:], 0, HALF)
         quantize(0, 0, N)
@@ -124,14 +125,16 @@ def tile_picked_tome_lin_none_sub_p_kernel(tc, x_words, x_scales, w, gate, offs,
         def entries(lo, hi):
             return offsets[:, lo // LIST_ROWS : hi // LIST_ROWS]
 
-        nc.scalar.activation(by_vector[:].indirect(entries(V, HALF)), gates[0][:, V:HALF], COPY)
+        nc.scalar.activation(by_vector[:].indirect(entries(0, V)), early_gates[:], COPY)
         sources = pool.tile([N, 3 * V], F32, name="sources", align_bytes=64)
         nc.vector.tensor_copy(
-            sources[:, V : 3 * V].rearrange("p (d v) -> p d v", v=V), acc[:].unsqueeze(1).to_broadcast([N, 2, V])
+            sources[:, 0:HALF].rearrange("p (d v) -> p d v", v=V), acc[:].unsqueeze(1).to_broadcast([N, 2, V])
         )
-        nc.vector.tensor_tensor(sources[:, 0:V], acc[:], gates[0][:, 0:V], MULT)
-        nc.scalar.activation(by_scalar[:].indirect(entries(0, HALF)), sources[:, 0:HALF], COPY)
-        nc.vector.tensor_tensor(by_vector[:].indirect(entries(HALF, S)), sources[:, V : 3 * V], gates[1][:], MULT)
+        nc.vector.tensor_tensor(sources[:, HALF : 3 * V], acc[:], late_gates[:, 0:V], MULT)
+        nc.scalar.activation(by_scalar[:].indirect(entries(0, HALF)), sources[:, V : 3 * V], COPY)
+        nc.vector.tensor_tensor(
+            by_vector[:].indirect(entries(HALF, S)), sources[:, 0:HALF], late_gates[:, V : 3 * V], MULT
+        )
         result = pool.tile([N, T], F32, name="result", align_bytes=64)
         for lo, hi in ((0, 128), (128, 320), (320, T)):
             nc.vector.tensor_tensor(result[:, lo:hi], by_scalar[:, lo:hi], by_vector[:, lo:hi], MULT)

@@ -13,7 +13,6 @@ U16 = mybir.dt.uint16
 U8 = mybir.dt.uint8
 FP8X4 = mybir.dt.float8_e4m3fn_x4
 MULT = mybir.AluOpType.mult
-ADD = mybir.AluOpType.add
 COPY = mybir.ActivationFunctionType.Copy
 
 P = 128
@@ -34,25 +33,23 @@ def tile_picked_tome_lin_none_sub_p_kernel(tc, x_words, x_scales, w, gate, offs,
         scales = pool.tile([P, 2 * T], U8, name="scales", align_bytes=64)
         w_raw = [pool.tile([P, PACK, N], F32, name=f"w_raw{d}", tag=f"slot{d}", align_bytes=64) for d in range(D)]
 
-        nc.vector.memset(scales[:, 0:T].bitcast(I32), 0)
+        def entries(lo, hi):
+            return offsets[:, lo // LIST_ROWS : hi // LIST_ROWS]
+
         scale_rows = x_scales[0].bitcast(I32)
-        early_scales = pool.tile([P, 2 * T], U8, name="early_scales", align_bytes=64)
-        nc.vector.memset(early_scales[:, 0:T].bitcast(I32), 0)
-        placed_scales = pool.tile([P, HALF], U8, name="placed_scales", align_bytes=64)
+        nc.scalar.dma_start(scales[16:32, 0:T].bitcast(I32), scale_rows)
+        nc.vector.memset(scales[0:16, 0:T].bitcast(I32), 0)
+        nc.vector.memset(scales[32:64, 0:T].bitcast(I32), 0)
+        nc.vector.memset(scales[64:P, 0:T].bitcast(I32), 0)
+        placed_scales = pool.tile([P, S], U8, name="placed_scales", align_bytes=64)
         nc.vector.memset(placed_scales[:].bitcast(I32), 0)
-        staged = pool.tile([16, T // 4], I32, name="staged", align_bytes=64)
-        nc.scalar.dma_start(staged[:], scale_rows)
-        nc.vector.tensor_copy(early_scales[0:16, 0:T].bitcast(I32), staged[:])
-        nc.vector.tensor_copy(scales[0:4, 0:T].bitcast(I32), staged[0:4, :])
         nc.sync.dma_start(offsets[:], offs)
-        nc.sync.dma_start(words[:, 0:T], x_words[0].rearrange("p c r -> p (c r)").bitcast(I32))
 
         def load_w(d):
             nc.sync.dma_start(w_raw[d][:], w[d].rearrange("(p j) m -> p j m", j=PACK))
 
         load_w(0)
-        for q in range(1, 4):
-            nc.sync.dma_start(scales[32 * q : 32 * q + 4, 0:T].bitcast(I32), scale_rows[4 * q : 4 * (q + 1), :])
+        nc.sync.dma_start(words[:, 0:T], x_words[0].rearrange("p c r -> p (c r)").bitcast(I32))
         for d in range(1, D):
             load_w(d)
         early_gates = pool.tile([P, V], F32, name="early_gates", align_bytes=64)
@@ -60,12 +57,7 @@ def tile_picked_tome_lin_none_sub_p_kernel(tc, x_words, x_scales, w, gate, offs,
         nc.sync.dma_start(early_gates[:], gate[:, 0:V])
 
         picked_words = pool.tile([P, S], U32, name="picked_words", align_bytes=64)
-        picked_scales = pool.tile([P, HALF], U8, name="picked_scales", align_bytes=64)
-        picked_early = pool.tile([P, HALF], U8, name="picked_early", align_bytes=64)
-
-        def gather(picked, window, lo, hi):
-            cols = offsets[:, lo // LIST_ROWS : hi // LIST_ROWS]
-            nc.vector.tensor_copy(picked[:], window.indirect(cols))
+        picked_scales = pool.tile([P, S], U8, name="picked_scales", align_bytes=64)
 
         grouped = pool.tile([P, D, N, PACK], BF16, name="grouped", align_bytes=64)
         w_codes = {}
@@ -90,14 +82,14 @@ def tile_picked_tome_lin_none_sub_p_kernel(tc, x_words, x_scales, w, gate, offs,
         for d in range(D - 1):
             interleave(nc.scalar.copy, d, 0, N)
         interleave(nc.scalar.copy, D - 1, VEC_COLS, N)
-        gather(picked_early, early_scales[:], HALF, S)
+        nc.vector.tensor_copy(picked_scales[:], scales[:].indirect(entries(0, S)))
         for q in range(4):
             nc.sync.dma_start(
-                placed_scales[32 * q : 32 * q + 4, :].bitcast(I32), picked_early[4 * q : 4 * q + 4, :].bitcast(I32)
+                placed_scales[32 * q : 32 * q + 4, :].bitcast(I32),
+                picked_scales[16 + 4 * q : 20 + 4 * q, :].bitcast(I32),
             )
         nc.sync.dma_start(late_gates[:], gate[:, V:S])
-        gather(picked_words, words[:].bitcast(U32), 0, S)
-        gather(picked_scales, scales[:], 0, HALF)
+        nc.vector.tensor_copy(picked_words[:], words[:].bitcast(U32).indirect(entries(0, S)))
         quantize(0, 0, N)
         quantize(1, 0, N)
         interleave(nc.vector.tensor_copy, D - 1, 0, VEC_COLS)
@@ -112,7 +104,7 @@ def tile_picked_tome_lin_none_sub_p_kernel(tc, x_words, x_scales, w, gate, offs,
                 lhsT=w_codes[d][:].bitcast(FP8X4),
                 lhsT_scale=w_scales[:, d * N : (d + 1) * N],
                 rhs=picked_words[:, d * V : (d + 1) * V].bitcast(FP8X4),
-                rhs_scale=(picked_scales, placed_scales)[d // 2][:, d % 2 * V : (d % 2 + 1) * V],
+                rhs_scale=placed_scales[:, d * V : (d + 1) * V],
                 start=(d == 0),
                 stop=(d == D - 1),
             )
@@ -121,9 +113,6 @@ def tile_picked_tome_lin_none_sub_p_kernel(tc, x_words, x_scales, w, gate, offs,
         by_vector = pool.tile([N, T], F32, name="by_vector", align_bytes=64)
         nc.vector.memset(by_scalar[:], 1.0)
         nc.vector.memset(by_vector[:], 1.0)
-
-        def entries(lo, hi):
-            return offsets[:, lo // LIST_ROWS : hi // LIST_ROWS]
 
         nc.scalar.activation(by_vector[:].indirect(entries(0, V)), early_gates[:], COPY)
         sources = pool.tile([N, 3 * V], F32, name="sources", align_bytes=64)

@@ -18,8 +18,9 @@ COPY = mybir.ActivationFunctionType.Copy
 P = 128
 PACK = 4
 LIST_ROWS = 16
+QUADS = 4
+QUAD_ROWS = 4
 HALF = S // 2
-VEC_COLS = 64
 
 
 def tile_picked_tome_lin_none_sub_p_kernel(tc, x_words, x_scales, w, gate, offs, out):
@@ -36,66 +37,58 @@ def tile_picked_tome_lin_none_sub_p_kernel(tc, x_words, x_scales, w, gate, offs,
         def entries(lo, hi):
             return offsets[:, lo // LIST_ROWS : hi // LIST_ROWS]
 
-        scale_rows = x_scales[0].bitcast(I32)
-        nc.scalar.dma_start(scales[16:32, 0:T].bitcast(I32), scale_rows)
-        nc.vector.memset(scales[0:16, 0:T].bitcast(I32), 0)
-        nc.vector.memset(scales[32:64, 0:T].bitcast(I32), 0)
-        nc.vector.memset(scales[64:P, 0:T].bitcast(I32), 0)
-        placed_scales = pool.tile([P, S], U8, name="placed_scales", align_bytes=64)
-        nc.vector.memset(placed_scales[:].bitcast(I32), 0)
-        nc.sync.dma_start(offsets[:], offs)
-
         def load_w(d):
             nc.sync.dma_start(w_raw[d][:], w[d].rearrange("(p j) m -> p j m", j=PACK))
 
-        load_w(0)
+        scale_rows = x_scales[0].bitcast(I32)
+        nc.vector.memset(scales[:, 0:T].bitcast(I32), 0)
+        nc.sync.dma_start(offsets[:], offs)
         nc.sync.dma_start(words[:, 0:T], x_words[0].rearrange("p c r -> p (c r)").bitcast(I32))
+        load_w(0)
+        for q in range(QUADS):
+            nc.sync.dma_start(
+                scales[32 * q : 32 * q + QUAD_ROWS, 0:T].bitcast(I32), scale_rows[QUAD_ROWS * q : QUAD_ROWS * (q + 1), :]
+            )
         for d in range(1, D):
             load_w(d)
         early_gates = pool.tile([P, V], F32, name="early_gates", align_bytes=64)
         late_gates = pool.tile([P, S - V], F32, name="late_gates", align_bytes=64)
         nc.sync.dma_start(early_gates[:], gate[:, 0:V])
+        nc.sync.dma_start(late_gates[:, 0:V], gate[:, V:HALF])
+        nc.sync.dma_start(late_gates[:, V : 3 * V], gate[:, HALF:S])
 
         picked_words = pool.tile([P, S], U32, name="picked_words", align_bytes=64)
         picked_scales = pool.tile([P, S], U8, name="picked_scales", align_bytes=64)
 
-        grouped = pool.tile([P, D, N, PACK], BF16, name="grouped", align_bytes=64)
-        w_codes = {}
+        w_codes = [pool.tile([P, N], U32, name=f"w_codes{d}", align_bytes=64) for d in range(D)]
         w_scales = pool.tile([P, D * N], U8, name="w_scales", align_bytes=64)
+        grouped = {}
 
-        def interleave(copy, d, lo, hi):
+        def interleave(copy, d, lo, hi, tag=None):
+            grouped[d, lo] = pool.tile([P, hi - lo, PACK], BF16, name=f"grouped{d}_{lo}", tag=tag or f"grouped{d}_{lo}", align_bytes=64)
             copy(
-                grouped[:, d, lo:hi, :].rearrange("p (c i) j -> p c j i", i=4),
+                grouped[d, lo][:].rearrange("p (c i) j -> p c j i", i=4),
                 w_raw[d][:, :, lo:hi].rearrange("p j (c i) -> p c j i", i=4),
             )
 
         def quantize(d, lo, hi):
-            if d not in w_codes:
-                tag = "slot2" if d == D - 1 else f"w_codes{d}"
-                w_codes[d] = pool.tile([P, N], U32, name=f"w_codes{d}", tag=tag, align_bytes=64)
             nc.vector.quantize_mx(
                 out=w_codes[d][:, lo:hi].bitcast(FP8X4),
                 scales=w_scales[:, d * N + lo : d * N + hi],
-                in_=grouped[:, d, lo:hi, :].rearrange("p m j -> p (m j)"),
+                in_=grouped[d, lo][:].rearrange("p m j -> p (m j)"),
             )
 
         for d in range(D - 1):
             interleave(nc.scalar.copy, d, 0, N)
-        interleave(nc.scalar.copy, D - 1, VEC_COLS, N)
-        nc.vector.tensor_copy(picked_scales[:], scales[:].indirect(entries(0, S)))
-        for q in range(4):
-            nc.sync.dma_start(
-                placed_scales[32 * q : 32 * q + 4, :].bitcast(I32),
-                picked_scales[16 + 4 * q : 20 + 4 * q, :].bitcast(I32),
-            )
-        nc.sync.dma_start(late_gates[:], gate[:, V:S])
+        interleave(nc.scalar.copy, D - 1, N // 2, N)
         nc.vector.tensor_copy(picked_words[:], words[:].bitcast(U32).indirect(entries(0, S)))
+        nc.vector.tensor_copy(picked_scales[:], scales[:].indirect(entries(0, S)))
         quantize(0, 0, N)
         quantize(1, 0, N)
-        interleave(nc.vector.tensor_copy, D - 1, 0, VEC_COLS)
+        interleave(nc.vector.tensor_copy, D - 1, 0, N // 2)
         quantize(2, 0, N)
-        quantize(3, 0, VEC_COLS)
-        quantize(3, VEC_COLS, N)
+        quantize(D - 1, 0, N // 2)
+        quantize(D - 1, N // 2, N)
 
         acc = psum.tile([N, V], F32, name="acc")
         for d in range(D):
@@ -104,7 +97,7 @@ def tile_picked_tome_lin_none_sub_p_kernel(tc, x_words, x_scales, w, gate, offs,
                 lhsT=w_codes[d][:].bitcast(FP8X4),
                 lhsT_scale=w_scales[:, d * N : (d + 1) * N],
                 rhs=picked_words[:, d * V : (d + 1) * V].bitcast(FP8X4),
-                rhs_scale=placed_scales[:, d * V : (d + 1) * V],
+                rhs_scale=picked_scales[:, d * V : (d + 1) * V],
                 start=(d == 0),
                 stop=(d == D - 1),
             )

@@ -42,8 +42,8 @@ def tile_picked_tome_lin_none_sub_p_kernel(tc, x_words, x_scales, w, gate, offs,
 
         scale_rows = x_scales[0].bitcast(I32)
         nc.vector.memset(scales[:, 0:T].bitcast(I32), 0)
-        nc.sync.dma_start(offsets[:], offs)
         nc.sync.dma_start(words[:, 0:T], x_words[0].rearrange("p c r -> p (c r)").bitcast(I32))
+        nc.sync.dma_start(offsets[:], offs)
         load_w(0)
         for q in range(QUADS):
             nc.sync.dma_start(

@@ -41,11 +41,13 @@ def tile_picked_tome_lin_none_sub_p_kernel(tc, x_words, x_scales, w, gate, offs,
             nc.sync.dma_start(w_raw[d][:], w[d].rearrange("(p j) m -> p j m", j=PACK))
 
         scale_rows = x_scales[0].bitcast(I32)
+        staged = pool.tile([QUAD_ROWS, T], U8, name="staged", align_bytes=64)
+        nc.scalar.dma_start(staged[:].bitcast(I32), scale_rows[0:QUAD_ROWS, :])
         nc.vector.memset(scales[:, 0:T].bitcast(I32), 0)
         nc.sync.dma_start(words[:, 0:T], x_words[0].rearrange("p c r -> p (c r)").bitcast(I32))
         nc.sync.dma_start(offsets[:], offs)
         load_w(0)
-        for q in range(QUADS):
+        for q in range(1, QUADS):
             nc.sync.dma_start(
                 scales[32 * q : 32 * q + QUAD_ROWS, 0:T].bitcast(I32), scale_rows[QUAD_ROWS * q : QUAD_ROWS * (q + 1), :]
             )
@@ -81,6 +83,7 @@ def tile_picked_tome_lin_none_sub_p_kernel(tc, x_words, x_scales, w, gate, offs,
         for d in range(D - 1):
             interleave(nc.scalar.copy, d, 0, N)
         interleave(nc.scalar.copy, D - 1, N // 2, N)
+        nc.vector.tensor_copy(scales[0:QUAD_ROWS, 0:T].bitcast(I32), staged[:].bitcast(I32))
         nc.vector.tensor_copy(picked_words[:], words[:].bitcast(U32).indirect(entries(0, S)))
         nc.vector.tensor_copy(picked_scales[:], scales[:].indirect(entries(0, S)))
         quantize(0, 0, N)

from contextlib import ExitStack

import concourse.mybir as mybir

K, T, D, S, V, N = 512, 512, 4, 512, 128, 128
FLOPS = 2 * D * K * N * V

F32 = mybir.dt.float32
BF16 = mybir.dt.bfloat16
I32 = mybir.dt.int32
U32 = mybir.dt.uint32
U16 = mybir.dt.uint16
U8 = mybir.dt.uint8
FP8X4 = mybir.dt.float8_e4m3fn_x4
MULT = mybir.AluOpType.mult
COPY = mybir.ActivationFunctionType.Copy

P = 128
PACK = 4
LIST_ROWS = 16
QUADS = 4
QUAD_ROWS = 4
HALF = S // 2


def tile_picked_tome_lin_none_sub_p_kernel(tc, x_words, x_scales, w, gate, offs, out):
    nc = tc.nc
    with ExitStack() as ctx:
        pool = ctx.enter_context(tc.tile_pool(name="sbuf", bufs=1))
        psum = ctx.enter_context(tc.psum_pool(name="psum", bufs=1))

        offsets = pool.tile([P, S // LIST_ROWS], U16, name="offsets")
        words = pool.tile([P, 2 * T], I32, name="words", align_bytes=64)
        scales = pool.tile([P, 2 * T], U8, name="scales", align_bytes=64)
        w_raw = [pool.tile([P, PACK, N], F32, name=f"w_raw{d}", tag=f"slot{d}", align_bytes=64) for d in range(D)]

        def entries(lo, hi):
            return offsets[:, lo // LIST_ROWS : hi // LIST_ROWS]

        def load_w(d):
            nc.sync.dma_start(w_raw[d][:], w[d].rearrange("(p j) m -> p j m", j=PACK))

        scale_rows = x_scales[0].bitcast(I32)
        staged = pool.tile([QUAD_ROWS, T], U8, name="staged", align_bytes=64)
        nc.scalar.dma_start(staged[:].bitcast(I32), scale_rows[0:QUAD_ROWS, :])
        nc.vector.memset(scales[:, 0:T].bitcast(I32), 0)
        nc.sync.dma_start(words[:, 0:T], x_words[0].rearrange("p c r -> p (c r)").bitcast(I32))
        nc.sync.dma_start(offsets[:], offs)
        load_w(0)
        for q in range(1, QUADS):
            nc.sync.dma_start(
                scales[32 * q : 32 * q + QUAD_ROWS, 0:T].bitcast(I32), scale_rows[QUAD_ROWS * q : QUAD_ROWS * (q + 1), :]
            )
        for d in range(1, D):
            load_w(d)
        early_gates = pool.tile([P, V], F32, name="early_gates", align_bytes=64)
        late_gates = pool.tile([P, S - V], F32, name="late_gates", align_bytes=64)
        nc.sync.dma_start(early_gates[:], gate[:, 0:V])
        nc.sync.dma_start(late_gates[:, 0:V], gate[:, V:HALF])
        nc.sync.dma_start(late_gates[:, V : 3 * V], gate[:, HALF:S])

        picked_words = pool.tile([P, S], U32, name="picked_words", align_bytes=64)
        picked_scales = pool.tile([P, S], U8, name="picked_scales", align_bytes=64)

        w_codes = [pool.tile([P, N], U32, name=f"w_codes{d}", align_bytes=64) for d in range(D)]
        w_scales = pool.tile([P, D * N], U8, name="w_scales", align_bytes=64)
        grouped = {}

        def interleave(copy, d, lo, hi, tag=None):
            grouped[d, lo] = pool.tile([P, hi - lo, PACK], BF16, name=f"grouped{d}_{lo}", tag=tag or f"grouped{d}_{lo}", align_bytes=64)
            copy(
                grouped[d, lo][:].rearrange("p (c i) j -> p c j i", i=4),
                w_raw[d][:, :, lo:hi].rearrange("p j (c i) -> p c j i", i=4),
            )

        def quantize(d, lo, hi):
            nc.vector.quantize_mx(
                out=w_codes[d][:, lo:hi].bitcast(FP8X4),
                scales=w_scales[:, d * N + lo : d * N + hi],
                in_=grouped[d, lo][:].rearrange("p m j -> p (m j)"),
            )

        for d in range(D - 1):
            interleave(nc.scalar.copy, d, 0, N)
        interleave(nc.scalar.copy, D - 1, N // 2, N)
        nc.vector.tensor_copy(scales[0:QUAD_ROWS, 0:T].bitcast(I32), staged[:].bitcast(I32))
        nc.vector.tensor_copy(picked_words[:], words[:].bitcast(U32).indirect(entries(0, S)))
        nc.vector.tensor_copy(picked_scales[:], scales[:].indirect(entries(0, S)))
        quantize(0, 0, N)
        quantize(1, 0, N)
        interleave(nc.vector.tensor_copy, D - 1, 0, N // 2)
        quantize(2, 0, N)
        quantize(D - 1, 0, N // 2)
        quantize(D - 1, N // 2, N)

        acc = psum.tile([N, V], F32, name="acc")
        for d in range(D):
            nc.tensor.matmul_mx(
                out=acc[:],
                lhsT=w_codes[d][:].bitcast(FP8X4),
                lhsT_scale=w_scales[:, d * N : (d + 1) * N],
                rhs=picked_words[:, d * V : (d + 1) * V].bitcast(FP8X4),
                rhs_scale=picked_scales[:, d * V : (d + 1) * V],
                start=(d == 0),
                stop=(d == D - 1),
            )

        by_scalar = pool.tile([N, T], F32, name="by_scalar", align_bytes=64)
        by_vector = pool.tile([N, T], F32, name="by_vector", align_bytes=64)
        nc.vector.memset(by_scalar[:], 1.0)
        nc.vector.memset(by_vector[:], 1.0)

        nc.scalar.activation(by_vector[:].indirect(entries(0, V)), early_gates[:], COPY)
        sources = pool.tile([N, 3 * V], F32, name="sources", align_bytes=64)
        nc.vector.tensor_copy(
            sources[:, 0:HALF].rearrange("p (d v) -> p d v", v=V), acc[:].unsqueeze(1).to_broadcast([N, 2, V])
        )
        nc.vector.tensor_tensor(sources[:, HALF : 3 * V], acc[:], late_gates[:, 0:V], MULT)
        nc.scalar.activation(by_scalar[:].indirect(entries(0, HALF)), sources[:, V : 3 * V], COPY)
        nc.vector.tensor_tensor(
            by_vector[:].indirect(entries(HALF, S)), sources[:, 0:HALF], late_gates[:, V : 3 * V], MULT
        )
        result = pool.tile([N, T], F32, name="result", align_bytes=64)
        for lo, hi in ((0, 128), (128, 320), (320, T)):
            nc.vector.tensor_tensor(result[:, lo:hi], by_scalar[:, lo:hi], by_vector[:, lo:hi], MULT)
            nc.sync.dma_start(out[:, lo:hi], result[:, lo:hi])
